import numpy as np
import ml_dtypes


def mxq(x, axis, fmt="e4m3"):
    dtype, down = {"e4m3": (ml_dtypes.float8_e4m3fn, 7), "e5m2": (ml_dtypes.float8_e5m2, 14)}[fmt]
    v = np.moveaxis(np.asarray(x, np.float32).astype(ml_dtypes.bfloat16).astype(np.float64), axis, -1)
    blocks = v.reshape(v.shape[:-1] + (-1, 32))
    amax = np.abs(blocks).max(-1, keepdims=True)
    byte = np.maximum(np.where(amax > 0, np.frexp(amax)[1] - 1 + 127, 0) - down, 1)
    scale = np.exp2(byte - 127.0)
    codes = (blocks / scale).astype(np.float32).astype(dtype).astype(np.float64)
    return np.moveaxis((codes * scale).reshape(v.shape), -1, axis)


WIDE = False


def mx_kscale(k):
    if not WIDE:
        return np.ones(k)
    levels = np.array([10, -10, 5, -5, 0])
    if k % 512:
        return np.exp2(np.random.permutation(np.resize(levels, k // 32))).repeat(32)
    a = np.empty((k // 512, 16))
    for p in range(k // 512):
        a[p, :8] = np.random.permutation(np.resize(levels, 8))
        for g in range(8):
            far = levels[np.abs(levels - a[p, g]) >= 10]
            a[p, g + 8] = far[np.random.randint(len(far))]
    return np.exp2(a.ravel()).repeat(32)


def f64(x):
    return np.asarray(x).astype(np.float64)


def striped(idx):
    return np.tile(idx.reshape(-1, 16).T, (8, 1)).astype(np.uint16)


def unstriped(offs):
    return offs[:16].T.reshape(-1).astype(np.int64)


E2M1 = np.array([0.0, 0.5, 1.0, 1.5, 2.0, 3.0, 4.0, 6.0, -0.0, -0.5, -1.0, -1.5, -2.0, -3.0, -4.0, -6.0])


def pack_weight(w, fmt):
    k, n = w.shape
    w = f64(np.asarray(w, np.float32).astype(ml_dtypes.bfloat16)).reshape(k // 32, 32, n)
    amax = np.abs(w).max(1)
    if fmt == "e4m3":
        byte = np.frexp(amax)[1] - 1 + 127 - 7
    else:
        mant, ex = np.frexp(amax / 6.0)
        byte = np.where(mant > 0.5, ex, ex - 1) + 127
    byte = np.clip(np.where(amax > 0, byte, 1), 1, 254)
    scaled = (w * np.exp2(127.0 - byte)[:, None, :]).reshape(k, n).astype(np.float32)
    by_word = np.ascontiguousarray(scaled.reshape(k // 512, 128, 4, n).transpose(0, 1, 3, 2))
    if fmt == "e4m3":
        words = by_word.astype(ml_dtypes.float8_e4m3fn).view(np.uint8)
    else:
        c = by_word.astype(ml_dtypes.float4_e2m1fn).view(np.uint8) & 0xF
        words = (c[..., 0::2] | (c[..., 1::2] << 4)).reshape(k // 512, 128, 2 * n)
    return np.ascontiguousarray(words), np.ascontiguousarray(byte.astype(np.uint8).reshape(k // 512, 16, n))


def unpack_weight(words, scales, fmt):
    g, _, n = scales.shape
    words = np.ascontiguousarray(words).reshape(g, 128, n, -1)
    if fmt == "e4m3":
        vals = words.view(ml_dtypes.float8_e4m3fn).astype(np.float64)
    else:
        nib = np.empty((g, 128, n, 4), np.uint8)
        nib[..., 0::2] = words & 0xF
        nib[..., 1::2] = words >> 4
        vals = E2M1[nib]
    vals = vals * np.repeat(np.exp2(scales.astype(np.float64) - 127.0), 8, axis=1)[..., None]
    return vals.transpose(0, 1, 3, 2).reshape(g * 512, n)


def silu(v):
    return v / (1.0 + np.exp(-np.maximum(v, -700.0)))


K, T, E, C, H, N = 1024, 768, 2, 256, 1024, 256


def by_expert(wq, xq):
    return np.concatenate([wq[e].T @ xq[:, e * C:(e + 1) * C] for e in range(E)], axis=1)


def setup_inputs():
    n = np.random.standard_normal
    s = mx_kscale(K)[:, None]
    u = mx_kscale(H)
    w1 = [pack_weight(m, "e2m1") for m in n((E, K, H)) / np.sqrt(K) / s[None]]
    w3 = [pack_weight(m, "e2m1") for m in n((E, K, H)) / np.sqrt(K) / s[None] * u[None, None, :]]
    w2 = [pack_weight(m, "e2m1") for m in n((E, H, N)) / np.sqrt(H) / u[None, :, None]]
    return {
        "xT": (n((K, T)) * s).astype(np.float32),
        "xr": n((N, T)).astype(np.float32),
        "w1_words": np.stack([m[0] for m in w1]),
        "w1_scales": np.stack([m[1] for m in w1]),
        "w3_words": np.stack([m[0] for m in w3]),
        "w3_scales": np.stack([m[1] for m in w3]),
        "w2_words": np.stack([m[0] for m in w2]),
        "w2_scales": np.stack([m[1] for m in w2]),
        "gate": np.tile(np.random.uniform(0.2, 1.0, E * C), (N, 1)).astype(np.float32),
        "offs": striped(np.random.permutation(T)[:E * C]),
    }


def reference(xT, xr, w1_words, w1_scales, w3_words, w3_scales, w2_words, w2_scales, gate, offs):
    idx = unstriped(offs)
    w1 = np.stack([unpack_weight(w1_words[e], w1_scales[e], "e2m1") for e in range(E)])
    w3 = np.stack([unpack_weight(w3_words[e], w3_scales[e], "e2m1") for e in range(E)])
    w2 = np.stack([unpack_weight(w2_words[e], w2_scales[e], "e2m1") for e in range(E)])
    xq = mxq(f64(xT)[:, idx], 0, "e4m3")
    h = silu(by_expert(w1, xq))
    h = h * by_expert(w3, xq)
    y = by_expert(w2, mxq(h, 0, "e4m3"))
    out = f64(xr).copy()
    out[:, idx] += f64(gate) * y
    return out

@@ -1,0 +1,230 @@
+from contextlib import ExitStack
+
+import concourse.mybir as mybir
+from concourse.masks import make_identity
+
+K, T, E, C, H, N = 1024, 768, 2, 256, 1024, 256
+SLOTS = E * C
+FLOPS = 2 * SLOTS * (2 * K * H + H * N)
+
+F32 = mybir.dt.float32
+BF16 = mybir.dt.bfloat16
+U32 = mybir.dt.uint32
+I32 = mybir.dt.int32
+U16 = mybir.dt.uint16
+U8 = mybir.dt.uint8
+FP8X4 = mybir.dt.float8_e4m3fn_x4
+FP4X4 = mybir.dt.float4_e2m1fn_x4
+MULT, ADD = mybir.AluOpType.mult, mybir.AluOpType.add
+SILU = mybir.ActivationFunctionType.Silu
+
+P = 128
+KP = 512
+PASSES = K // KP
+G = H // KP
+UNITS = SLOTS // P
+NT = N // P
+CHUNKS = (((0, 256, 96), (256, 512, 64)), ((0, 512, 64), (512, 256, 128)))
+
+
+def tile_moe_res_glu_silu_kernel(
+    tc, xT, xr, w1_words, w1_scales, w3_words, w3_scales, w2_words, w2_scales, gate, offs, out
+):
+    nc = tc.nc
+    with ExitStack() as ctx:
+        keep = ctx.enter_context(tc.tile_pool(name="keep", bufs=1))
+        ring = ctx.enter_context(tc.tile_pool(name="ring", bufs=2))
+        psum = ctx.enter_context(tc.psum_pool(name="psum", bufs=1))
+
+        offsets = keep.tile([P, SLOTS // 16], U16, name="offsets")
+        nc.sync.dma_start(offsets[:], offs)
+
+        codes, sbytes, xq, xs = {}, {}, {}, {}
+        for s in range(PASSES):
+            codes[s] = keep.tile([P, T], U32, name=f"codes{s}", align_bytes=64)
+            sbytes[s] = keep.tile([P, T], U8, name=f"bytes{s}", align_bytes=64)
+            nc.gpsimd.memset(sbytes[s][:], 0)
+            for e in range(E):
+                xq[s, e] = keep.tile([P, C], U32, name=f"xq{s}{e}", align_bytes=64)
+                xs[s, e] = keep.tile([P, C], U8, name=f"xs{s}{e}", align_bytes=64)
+
+        warm = keep.tile([P, 1], F32, name="warm")
+        nc.vector.memset(warm[:], 0.0)
+        nc.scalar.activation(warm[:], warm[:], SILU)
+        ident = keep.tile([P, P], F32, name="ident")
+        words = (w1_words, w3_words)
+        wscales = (w1_scales, w3_scales)
+        wsc = {}
+        for m in range(2):
+            wsc[m] = keep.tile([P, E * PASSES, H], U8, name=f"wsc{m}", align_bytes=64)
+            nc.vector.memset(wsc[m][:].rearrange("p s i -> p (s i)").bitcast(I32), 0)
+        w2sc = keep.tile([P, E, PASSES, N], U8, name="w2sc", align_bytes=64)
+        nc.vector.memset(w2sc[:].rearrange("p e s n -> p (e s n)").bitcast(I32), 0)
+
+        def load_scales(queue, m):
+            for q in range(4):
+                queue.dma_start(
+                    wsc[m][32 * q : 32 * q + 4, :, :].bitcast(I32),
+                    wscales[m][:, :, 4 * q : 4 * q + 4, :].rearrange("e s q i -> q (e s) i").bitcast(I32),
+                )
+
+        xview = xT.rearrange("(s p j) w -> s p j w", s=PASSES, p=P, j=4)
+        raw = {}
+
+        def load_x(s, i):
+            t0, tw, vcols = CHUNKS[s][i]
+            raw[s, i] = keep.tile([P, 4, tw], F32, name=f"raw{s}{i}")
+            nc.sync.dma_start(raw[s, i][:], xview[s][:, :, t0 : t0 + tw])
+
+        wt = {}
+
+        def load_words(e, m):
+            wt[e, m] = keep.tile([P, PASSES, 2 * H], U8, name=f"wt{e}{m}", align_bytes=64)
+            nc.sync.dma_start(wt[e, m][:].bitcast(I32), words[m][e].rearrange("s p b -> p s b").bitcast(I32))
+
+        load_x(0, 0)
+        load_x(0, 1)
+        load_scales(nc.sync, 0)
+        load_x(1, 0)
+        load_x(1, 1)
+        load_scales(nc.sync, 1)
+        load_words(0, 0)
+        load_words(0, 1)
+        for q in range(4):
+            nc.gpsimd.dma_start(
+                w2sc[32 * q : 32 * q + 4, :, :, :].rearrange("p e s n -> p (e s) n").bitcast(I32),
+                w2_scales[:, :, 4 * q : 4 * q + 4, :].rearrange("e s q n -> q (e s) n").bitcast(I32),
+            )
+        w2t = keep.tile([P, E, PASSES, 2 * N], U8, name="w2t", align_bytes=64)
+        nc.sync.dma_start(w2t[:].bitcast(I32), w2_words.rearrange("e s p b -> p e s b").bitcast(I32))
+        load_words(1, 0)
+        load_words(1, 1)
+        gates = keep.tile([P, SLOTS], F32, name="gates")
+        nc.sync.dma_start(gates[:], gate[0:P, :])
+        res_in = {}
+        for n in range(NT):
+            res_in[n] = keep.tile([P, T], F32, name=f"res_in{n}")
+            nc.sync.dma_start(res_in[n][:], xr[n * P : (n + 1) * P, :])
+
+        make_identity(nc, ident[:])
+        back = {}
+        for n in range(NT):
+            back[n] = keep.tile([P, T], F32, name=f"back{n}")
+            nc.gpsimd.memset(back[n][:], 0.0)
+
+        def gather(s, e):
+            mine = offsets[:, e * C // 16 : (e + 1) * C // 16]
+            nc.vector.tensor_copy(xq[s, e][:], codes[s][:].indirect(mine))
+            nc.vector.tensor_copy(xs[s, e][:], sbytes[s][:].indirect(mine))
+
+        for s in range(PASSES):
+            for i, (t0, tw, v) in enumerate(CHUNKS[s]):
+                rounded = keep.tile([P, tw, 4], BF16, name=f"rounded{s}{i}", align_bytes=64)
+                dst = rounded[:].rearrange("p (c i) j -> p c j i", i=4)
+                src = raw[s, i][:].rearrange("p j (c i) -> p c j i", i=4)
+                nc.vector.tensor_copy(dst[:, 0 : v // 4], src[:, 0 : v // 4])
+                nc.scalar.copy(dst[:, v // 4 :], src[:, v // 4 :])
+                nc.vector.quantize_mx(
+                    out=codes[s][:, t0 : t0 + tw].bitcast(FP8X4),
+                    scales=sbytes[s][:, t0 : t0 + tw],
+                    in_=rounded[:].rearrange("p w j -> p (w j)"),
+                )
+            gather(s, 0)
+
+        def stage1(j):
+            e, c0 = j * P // C, j * P % C
+            cols = slice(c0, c0 + P)
+            acc = {}
+            for g in range(G):
+                for m in range(2):
+                    acc[g, m] = psum.tile([P, KP], F32, name=f"acc{g}{m}", tag="acc", bufs=5)
+            if j == 0:
+                order = [(g, m, s) for s in range(PASSES) for g in range(G) for m in range(2)]
+            else:
+                order = [(g, m, s) for g in range(G) for m in range(2) for s in range(PASSES)]
+            for g, m, s in order:
+                nc.tensor.matmul_mx(
+                    out=acc[g, m][:],
+                    lhsT=xq[s, e][:, cols].bitcast(FP8X4),
+                    lhsT_scale=xs[s, e][:, cols],
+                    rhs=wt[e, m][:, s, 2 * KP * g : 2 * KP * (g + 1)].bitcast(FP4X4),
+                    rhs_scale=wsc[m][:, e * PASSES + s, g * KP : (g + 1) * KP],
+                    start=(s == 0),
+                    stop=(s == PASSES - 1),
+                )
+            h = ring.tile([P, G, 2, P, 2], BF16, name="h", align_bytes=64)
+            for g in range(G):
+                act = ring.tile([P, KP], F32, name="act", bufs=3)
+                nc.scalar.activation(act[:], acc[g, 0][:], SILU)
+                nc.vector.tensor_tensor(
+                    h[:, g, :, :, :],
+                    act[:].rearrange("r (p u e) -> r u p e", u=2, e=2),
+                    acc[g, 1][:].rearrange("r (p u e) -> r u p e", u=2, e=2),
+                    MULT,
+                )
+            return h
+
+        def stage2(j, h, ys, at):
+            e = j * P // C
+            turned = psum.tile([P, G, 2, P], F32, name="turned", tag="turned", bufs=2)
+            hq_in = ring.tile([P, G, P, 4], BF16, name="hq_in", align_bytes=64)
+            hq = ring.tile([P, G, P], U32, name="hq", align_bytes=64)
+            hs = ring.tile([P, G, P], U8, name="hs", align_bytes=64)
+            hw = h[:].rearrange("r g u p e -> r (g u p e)").bitcast(F32)
+            for g in range(G):
+                for u in range(2):
+                    w0 = (2 * g + u) * P
+                    nc.tensor.transpose(turned[:, g, u, :], hw[:, w0 : w0 + P], ident[:])
+            nc.scalar.copy(
+                hq_in[:].rearrange("p g r t -> p (g r t)").bitcast(F32).rearrange("p (g r u) -> p g r u", g=G, u=2),
+                turned[:].rearrange("p g u r -> p g r u"),
+            )
+            nc.vector.quantize_mx(
+                out=hq[:].rearrange("p g r -> p (g r)").bitcast(FP8X4),
+                scales=hs[:].rearrange("p g r -> p (g r)"),
+                in_=hq_in[:].rearrange("p g r t -> p (g r t)"),
+            )
+            y = psum.tile([P, NT, P], F32, name="y", tag="y", bufs=1)
+            for n in range(NT):
+                for g in range(G):
+                    nc.tensor.matmul_mx(
+                        out=y[:, n, :],
+                        lhsT=w2t[:, e, g, 2 * P * n : 2 * P * (n + 1)].bitcast(FP4X4),
+                        lhsT_scale=w2sc[:, e, g, P * n : P * (n + 1)],
+                        rhs=hq[:, g, :].bitcast(FP8X4),
+                        rhs_scale=hs[:, g, :],
+                        start=(g == 0),
+                        stop=(g == G - 1),
+                    )
+            nc.scalar.copy(ys[:, :, at : at + P], y[:])
+
+        def scatter(ys, j0, width):
+            for n in range(NT):
+                nc.vector.tensor_tensor(
+                    back[n][:].indirect(offsets[:, j0 // 16 : (j0 + width) // 16]),
+                    ys[:, n, :],
+                    gates[:, j0 : j0 + width],
+                    MULT,
+                )
+
+        ys0 = keep.tile([P, NT, C], F32, name="ys0")
+        ys2 = keep.tile([P, NT, P], F32, name="ys2")
+        ys3 = keep.tile([P, NT, P], F32, name="ys3")
+        h0 = stage1(0)
+        for s in range(PASSES):
+            gather(s, 1)
+        h1 = stage1(1)
+        stage2(0, h0, ys0, 0)
+        h2 = stage1(2)
+        stage2(1, h1, ys0, P)
+        h3 = stage1(3)
+        stage2(2, h2, ys2, 0)
+        scatter(ys0, 0, C)
+        stage2(3, h3, ys3, 0)
+        scatter(ys2, C, P)
+        scatter(ys3, C + P, P)
+
+        for n in range(NT):
+            done = keep.tile([P, T], F32, name=f"done{n}")
+            nc.vector.tensor_tensor(done[:], back[n][:], res_in[n][:], ADD)
+            nc.sync.dma_start(out[n * P : (n + 1) * P, :], done[:])

@@ -24,7 +24,7 @@ PASSES = K // KP
 G = H // KP
 UNITS = SLOTS // P
 NT = N // P
-CHUNKS = (((0, 256, 96), (256, 512, 64)), ((0, 512, 64), (512, 256, 128)))
+VEC_COLS = {(0, 0): 256, (0, 1): 64, (1, 0): 64, (1, 1): 384}
 
 
 def tile_moe_res_glu_silu_kernel(
@@ -39,42 +39,34 @@ def tile_moe_res_glu_silu_kernel(
         offsets = keep.tile([P, SLOTS // 16], U16, name="offsets")
         nc.sync.dma_start(offsets[:], offs)
 
-        codes, sbytes, xq, xs = {}, {}, {}, {}
-        for s in range(PASSES):
-            codes[s] = keep.tile([P, T], U32, name=f"codes{s}", align_bytes=64)
-            sbytes[s] = keep.tile([P, T], U8, name=f"bytes{s}", align_bytes=64)
-            nc.gpsimd.memset(sbytes[s][:], 0)
-            for e in range(E):
-                xq[s, e] = keep.tile([P, C], U32, name=f"xq{s}{e}", align_bytes=64)
-                xs[s, e] = keep.tile([P, C], U8, name=f"xs{s}{e}", align_bytes=64)
-
         warm = keep.tile([P, 1], F32, name="warm")
         nc.vector.memset(warm[:], 0.0)
         nc.scalar.activation(warm[:], warm[:], SILU)
         ident = keep.tile([P, P], F32, name="ident")
+        make_identity(nc, ident[:])
         words = (w1_words, w3_words)
         wscales = (w1_scales, w3_scales)
         wsc = {}
-        for m in range(2):
-            wsc[m] = keep.tile([P, E * PASSES, H], U8, name=f"wsc{m}", align_bytes=64)
-            nc.vector.memset(wsc[m][:].rearrange("p s i -> p (s i)").bitcast(I32), 0)
+        for e in range(E):
+            for m in range(2):
+                wsc[e, m] = keep.tile([P, PASSES, H], U8, name=f"wsc{e}{m}", align_bytes=64)
+                nc.vector.memset(wsc[e, m][:].rearrange("p s i -> p (s i)").bitcast(I32), 0)
         w2sc = keep.tile([P, E, PASSES, N], U8, name="w2sc", align_bytes=64)
         nc.vector.memset(w2sc[:].rearrange("p e s n -> p (e s n)").bitcast(I32), 0)
 
-        def load_scales(queue, m):
+        def load_scales(queue, e, m):
             for q in range(4):
                 queue.dma_start(
-                    wsc[m][32 * q : 32 * q + 4, :, :].bitcast(I32),
-                    wscales[m][:, :, 4 * q : 4 * q + 4, :].rearrange("e s q i -> q (e s) i").bitcast(I32),
+                    wsc[e, m][32 * q : 32 * q + 4, :, :].bitcast(I32),
+                    wscales[m][e][:, 4 * q : 4 * q + 4, :].rearrange("s q i -> q s i").bitcast(I32),
                 )
 
-        xview = xT.rearrange("(s p j) w -> s p j w", s=PASSES, p=P, j=4)
+        xview = xT.rearrange("(s p u e) w -> s u p e w", s=PASSES, p=P, u=2, e=2)
         raw = {}
-
-        def load_x(s, i):
-            t0, tw, vcols = CHUNKS[s][i]
-            raw[s, i] = keep.tile([P, 4, tw], F32, name=f"raw{s}{i}")
-            nc.sync.dma_start(raw[s, i][:], xview[s][:, :, t0 : t0 + tw])
+        for s in range(PASSES):
+            for u in range(2):
+                raw[s, u] = keep.tile([P, 2, T], F32, name=f"raw{s}{u}")
+                nc.sync.dma_start(raw[s, u][:], xview[s, u])
 
         wt = {}
 
@@ -82,22 +74,20 @@ def tile_moe_res_glu_silu_kernel(
             wt[e, m] = keep.tile([P, PASSES, 2 * H], U8, name=f"wt{e}{m}", align_bytes=64)
             nc.sync.dma_start(wt[e, m][:].bitcast(I32), words[m][e].rearrange("s p b -> p s b").bitcast(I32))
 
-        load_x(0, 0)
-        load_x(0, 1)
-        load_scales(nc.sync, 0)
-        load_x(1, 0)
-        load_x(1, 1)
-        load_scales(nc.sync, 1)
-        load_words(0, 0)
-        load_words(0, 1)
+        load_scales(nc.sync, 0, 0)
+        load_scales(nc.gpsimd, 0, 1)
         for q in range(4):
             nc.gpsimd.dma_start(
                 w2sc[32 * q : 32 * q + 4, :, :, :].rearrange("p e s n -> p (e s) n").bitcast(I32),
                 w2_scales[:, :, 4 * q : 4 * q + 4, :].rearrange("e s q n -> q (e s) n").bitcast(I32),
             )
+        load_words(0, 0)
+        load_words(0, 1)
         w2t = keep.tile([P, E, PASSES, 2 * N], U8, name="w2t", align_bytes=64)
         nc.sync.dma_start(w2t[:].bitcast(I32), w2_words.rearrange("e s p b -> p e s b").bitcast(I32))
+        load_scales(nc.sync, 1, 0)
         load_words(1, 0)
+        load_scales(nc.sync, 1, 1)
         load_words(1, 1)
         gates = keep.tile([P, SLOTS], F32, name="gates")
         nc.sync.dma_start(gates[:], gate[0:P, :])
@@ -106,30 +96,37 @@ def tile_moe_res_glu_silu_kernel(
             res_in[n] = keep.tile([P, T], F32, name=f"res_in{n}")
             nc.sync.dma_start(res_in[n][:], xr[n * P : (n + 1) * P, :])
 
-        make_identity(nc, ident[:])
         back = {}
         for n in range(NT):
             back[n] = keep.tile([P, T], F32, name=f"back{n}")
             nc.gpsimd.memset(back[n][:], 0.0)
 
-        def gather(s, e):
-            mine = offsets[:, e * C // 16 : (e + 1) * C // 16]
-            nc.vector.tensor_copy(xq[s, e][:], codes[s][:].indirect(mine))
-            nc.vector.tensor_copy(xs[s, e][:], sbytes[s][:].indirect(mine))
+        xq, xs, grouped, pairs = {}, {}, {}, {}
+        for s in range(PASSES):
+            for e in range(E):
+                grouped[s, e] = keep.tile([P, C, 4], BF16, name=f"grouped{s}{e}", align_bytes=64)
+                xq[s, e] = keep.tile([P, C], U32, name=f"xq{s}{e}", align_bytes=64)
+                xs[s, e] = keep.tile([P, C], U8, name=f"xs{s}{e}", align_bytes=64)
+
+        def gather(s, u, e):
+            pair_out = grouped[s, e][:].rearrange("p r t -> p (r t)").bitcast(U32).rearrange("p (r u) -> p r u", u=2)
+            table = pairs[s, u][:].rearrange("p w e -> p (w e)").bitcast(U32)
+            nc.vector.tensor_copy(pair_out[:, :, u], table.indirect(offsets[:, e * C // 16 : (e + 1) * C // 16]))
+
+        def quantise(s, e):
+            nc.vector.quantize_mx(
+                out=xq[s, e][:].bitcast(FP8X4), scales=xs[s, e][:], in_=grouped[s, e][:].rearrange("p r t -> p (r t)")
+            )
 
         for s in range(PASSES):
-            for i, (t0, tw, v) in enumerate(CHUNKS[s]):
-                rounded = keep.tile([P, tw, 4], BF16, name=f"rounded{s}{i}", align_bytes=64)
-                dst = rounded[:].rearrange("p (c i) j -> p c j i", i=4)
-                src = raw[s, i][:].rearrange("p j (c i) -> p c j i", i=4)
-                nc.vector.tensor_copy(dst[:, 0 : v // 4], src[:, 0 : v // 4])
-                nc.scalar.copy(dst[:, v // 4 :], src[:, v // 4 :])
-                nc.vector.quantize_mx(
-                    out=codes[s][:, t0 : t0 + tw].bitcast(FP8X4),
-                    scales=sbytes[s][:, t0 : t0 + tw],
-                    in_=rounded[:].rearrange("p w j -> p (w j)"),
-                )
-            gather(s, 0)
+            for u in range(2):
+                pairs[s, u] = keep.tile([P, T, 2], BF16, name=f"pairs{s}{u}", align_bytes=64)
+                src = raw[s, u][:].rearrange("p e w -> p w e")
+                v = VEC_COLS[s, u]
+                nc.vector.tensor_copy(pairs[s, u][:, 0:v, :], src[:, 0:v, :])
+                nc.scalar.copy(pairs[s, u][:, v:T, :], src[:, v:T, :])
+                gather(s, u, 0)
+            quantise(s, 0)
 
         def stage1(j):
             e, c0 = j * P // C, j * P % C
@@ -148,7 +145,7 @@ def tile_moe_res_glu_silu_kernel(
                     lhsT=xq[s, e][:, cols].bitcast(FP8X4),
                     lhsT_scale=xs[s, e][:, cols],
                     rhs=wt[e, m][:, s, 2 * KP * g : 2 * KP * (g + 1)].bitcast(FP4X4),
-                    rhs_scale=wsc[m][:, e * PASSES + s, g * KP : (g + 1) * KP],
+                    rhs_scale=wsc[e, m][:, s, g * KP : (g + 1) * KP],
                     start=(s == 0),
                     stop=(s == PASSES - 1),
                 )
@@ -164,7 +161,7 @@ def tile_moe_res_glu_silu_kernel(
                 )
             return h
 
-        def stage2(j, h, ys, at):
+        def stage2(j, h, y_sb):
             e = j * P // C
             turned = psum.tile([P, G, 2, P], F32, name="turned", tag="turned", bufs=2)
             hq_in = ring.tile([P, G, P, 4], BF16, name="hq_in", align_bytes=64)
@@ -196,33 +193,31 @@ def tile_moe_res_glu_silu_kernel(
                         start=(g == 0),
                         stop=(g == G - 1),
                     )
-            nc.scalar.copy(ys[:, :, at : at + P], y[:])
+            nc.scalar.copy(y_sb[:], y[:])
 
-        def scatter(ys, j0, width):
+        def scatter(y_sb, j):
+            cols = slice(j * P, (j + 1) * P)
             for n in range(NT):
                 nc.vector.tensor_tensor(
-                    back[n][:].indirect(offsets[:, j0 // 16 : (j0 + width) // 16]),
-                    ys[:, n, :],
-                    gates[:, j0 : j0 + width],
-                    MULT,
+                    back[n][:].indirect(offsets[:, j * P // 16 : (j + 1) * P // 16]), y_sb[:, n, :], gates[:, cols], MULT
                 )
 
-        ys0 = keep.tile([P, NT, C], F32, name="ys0")
-        ys2 = keep.tile([P, NT, P], F32, name="ys2")
-        ys3 = keep.tile([P, NT, P], F32, name="ys3")
-        h0 = stage1(0)
+        ys = {j: keep.tile([P, NT, P], F32, name=f"ys{j}") for j in range(UNITS)}
+        h = {}
+        h[0] = stage1(0)
         for s in range(PASSES):
-            gather(s, 1)
-        h1 = stage1(1)
-        stage2(0, h0, ys0, 0)
-        h2 = stage1(2)
-        stage2(1, h1, ys0, P)
-        h3 = stage1(3)
-        stage2(2, h2, ys2, 0)
-        scatter(ys0, 0, C)
-        stage2(3, h3, ys3, 0)
-        scatter(ys2, C, P)
-        scatter(ys3, C + P, P)
+            for u in range(2):
+                gather(s, u, 1)
+            quantise(s, 1)
+        h[1] = stage1(1)
+        stage2(0, h[0], ys[0])
+        h[2] = stage1(2)
+        stage2(1, h[1], ys[1])
+        h[3] = stage1(3)
+        stage2(2, h[2], ys[2])
+        stage2(3, h[3], ys[3])
+        for j in range(UNITS):
+            scatter(ys[j], j)
 
         for n in range(NT):
             done = keep.tile([P, T], F32, name=f"done{n}")

@@ -24,7 +24,7 @@ PASSES = K // KP
 G = H // KP
 UNITS = SLOTS // P
 NT = N // P
-VEC_COLS = {(0, 0): 256, (0, 1): 64, (1, 0): 64, (1, 1): 384}
+VEC_COLS = {(0, 0): 256, (0, 1): 128, (1, 0): 192, (1, 1): 384}
 
 
 def tile_moe_res_glu_silu_kernel(
@@ -53,6 +53,10 @@ def tile_moe_res_glu_silu_kernel(
                 nc.vector.memset(wsc[e, m][:].rearrange("p s i -> p (s i)").bitcast(I32), 0)
         w2sc = keep.tile([P, E, PASSES, N], U8, name="w2sc", align_bytes=64)
         nc.vector.memset(w2sc[:].rearrange("p e s n -> p (e s n)").bitcast(I32), 0)
+        back = {}
+        for n in range(NT):
+            back[n] = keep.tile([P, T], F32, name=f"back{n}")
+            nc.vector.memset(back[n][:], 0.0)
 
         def load_scales(queue, e, m):
             for q in range(4):
@@ -63,10 +67,10 @@ def tile_moe_res_glu_silu_kernel(
 
         xview = xT.rearrange("(s p u e) w -> s u p e w", s=PASSES, p=P, u=2, e=2)
         raw = {}
-        for s in range(PASSES):
-            for u in range(2):
-                raw[s, u] = keep.tile([P, 2, T], F32, name=f"raw{s}{u}")
-                nc.sync.dma_start(raw[s, u][:], xview[s, u])
+
+        def load_x(s, u):
+            raw[s, u] = keep.tile([P, 2, T], F32, name=f"raw{s}{u}")
+            nc.sync.dma_start(raw[s, u][:], xview[s, u])
 
         wt = {}
 
@@ -74,32 +78,31 @@ def tile_moe_res_glu_silu_kernel(
             wt[e, m] = keep.tile([P, PASSES, 2 * H], U8, name=f"wt{e}{m}", align_bytes=64)
             nc.sync.dma_start(wt[e, m][:].bitcast(I32), words[m][e].rearrange("s p b -> p s b").bitcast(I32))
 
+        load_x(0, 0)
         load_scales(nc.sync, 0, 0)
-        load_scales(nc.gpsimd, 0, 1)
-        for q in range(4):
-            nc.gpsimd.dma_start(
-                w2sc[32 * q : 32 * q + 4, :, :, :].rearrange("p e s n -> p (e s) n").bitcast(I32),
-                w2_scales[:, :, 4 * q : 4 * q + 4, :].rearrange("e s q n -> q (e s) n").bitcast(I32),
-            )
+        load_x(0, 1)
+        load_x(1, 0)
+        load_x(1, 1)
         load_words(0, 0)
+        load_scales(nc.sync, 0, 1)
         load_words(0, 1)
         w2t = keep.tile([P, E, PASSES, 2 * N], U8, name="w2t", align_bytes=64)
         nc.sync.dma_start(w2t[:].bitcast(I32), w2_words.rearrange("e s p b -> p e s b").bitcast(I32))
-        load_scales(nc.sync, 1, 0)
         load_words(1, 0)
-        load_scales(nc.sync, 1, 1)
         load_words(1, 1)
+        for m in range(2):
+            load_scales(nc.gpsimd, 1, m)
+        for q in range(4):
+            nc.sync.dma_start(
+                w2sc[32 * q : 32 * q + 4, :, :, :].rearrange("p e s n -> p (e s) n").bitcast(I32),
+                w2_scales[:, :, 4 * q : 4 * q + 4, :].rearrange("e s q n -> q (e s) n").bitcast(I32),
+            )
         gates = keep.tile([P, SLOTS], F32, name="gates")
         nc.sync.dma_start(gates[:], gate[0:P, :])
         res_in = {}
         for n in range(NT):
             res_in[n] = keep.tile([P, T], F32, name=f"res_in{n}")
             nc.sync.dma_start(res_in[n][:], xr[n * P : (n + 1) * P, :])
-
-        back = {}
-        for n in range(NT):
-            back[n] = keep.tile([P, T], F32, name=f"back{n}")
-            nc.gpsimd.memset(back[n][:], 0.0)
 
         xq, xs, grouped, pairs = {}, {}, {}, {}
         for s in range(PASSES):

@@ -24,7 +24,7 @@ PASSES = K // KP
 G = H // KP
 UNITS = SLOTS // P
 NT = N // P
-VEC_COLS = {(0, 0): 256, (0, 1): 128, (1, 0): 192, (1, 1): 384}
+VEC_COLS = {(0, 0): 384, (0, 1): 256, (1, 0): 256, (1, 1): 384}
 
 
 def tile_moe_res_glu_silu_kernel(
@@ -45,24 +45,22 @@ def tile_moe_res_glu_silu_kernel(
         ident = keep.tile([P, P], F32, name="ident")
         make_identity(nc, ident[:])
         words = (w1_words, w3_words)
-        wscales = (w1_scales, w3_scales)
-        wsc = {}
-        for e in range(E):
-            for m in range(2):
-                wsc[e, m] = keep.tile([P, PASSES, H], U8, name=f"wsc{e}{m}", align_bytes=64)
-                nc.vector.memset(wsc[e, m][:].rearrange("p s i -> p (s i)").bitcast(I32), 0)
         w2sc = keep.tile([P, E, PASSES, N], U8, name="w2sc", align_bytes=64)
         nc.vector.memset(w2sc[:].rearrange("p e s n -> p (e s n)").bitcast(I32), 0)
+        wsc = {}
+        for m in range(2):
+            wsc[m] = keep.tile([P, E, PASSES, H], U8, name=f"wsc{m}", align_bytes=64)
+            nc.vector.memset(wsc[m][:].rearrange("p e s i -> p (e s i)").bitcast(I32), 0)
         back = {}
         for n in range(NT):
             back[n] = keep.tile([P, T], F32, name=f"back{n}")
             nc.vector.memset(back[n][:], 0.0)
 
-        def load_scales(queue, e, m):
+        def load_scales(plane, scales):
             for q in range(4):
-                queue.dma_start(
-                    wsc[e, m][32 * q : 32 * q + 4, :, :].bitcast(I32),
-                    wscales[m][e][:, 4 * q : 4 * q + 4, :].rearrange("s q i -> q s i").bitcast(I32),
+                nc.sync.dma_start(
+                    plane[32 * q : 32 * q + 4].rearrange("p e s i -> p (e s) i").bitcast(I32),
+                    scales[:, :, 4 * q : 4 * q + 4, :].rearrange("e s q i -> q (e s) i").bitcast(I32),
                 )
 
         xview = xT.rearrange("(s p u e) w -> s u p e w", s=PASSES, p=P, u=2, e=2)
@@ -79,24 +77,18 @@ def tile_moe_res_glu_silu_kernel(
             nc.sync.dma_start(wt[e, m][:].bitcast(I32), words[m][e].rearrange("s p b -> p s b").bitcast(I32))
 
         load_x(0, 0)
-        load_scales(nc.sync, 0, 0)
+        load_scales(w2sc, w2_scales)
         load_x(0, 1)
         load_x(1, 0)
         load_x(1, 1)
+        load_scales(wsc[0], w1_scales)
         load_words(0, 0)
-        load_scales(nc.sync, 0, 1)
         load_words(0, 1)
+        load_scales(wsc[1], w3_scales)
         w2t = keep.tile([P, E, PASSES, 2 * N], U8, name="w2t", align_bytes=64)
         nc.sync.dma_start(w2t[:].bitcast(I32), w2_words.rearrange("e s p b -> p e s b").bitcast(I32))
         load_words(1, 0)
         load_words(1, 1)
-        for m in range(2):
-            load_scales(nc.gpsimd, 1, m)
-        for q in range(4):
-            nc.sync.dma_start(
-                w2sc[32 * q : 32 * q + 4, :, :, :].rearrange("p e s n -> p (e s) n").bitcast(I32),
-                w2_scales[:, :, 4 * q : 4 * q + 4, :].rearrange("e s q n -> q (e s) n").bitcast(I32),
-            )
         gates = keep.tile([P, SLOTS], F32, name="gates")
         nc.sync.dma_start(gates[:], gate[0:P, :])
         res_in = {}
@@ -121,15 +113,29 @@ def tile_moe_res_glu_silu_kernel(
                 out=xq[s, e][:].bitcast(FP8X4), scales=xs[s, e][:], in_=grouped[s, e][:].rearrange("p r t -> p (r t)")
             )
 
-        for s in range(PASSES):
-            for u in range(2):
-                pairs[s, u] = keep.tile([P, T, 2], BF16, name=f"pairs{s}{u}", align_bytes=64)
-                src = raw[s, u][:].rearrange("p e w -> p w e")
-                v = VEC_COLS[s, u]
-                nc.vector.tensor_copy(pairs[s, u][:, 0:v, :], src[:, 0:v, :])
-                nc.scalar.copy(pairs[s, u][:, v:T, :], src[:, v:T, :])
-                gather(s, u, 0)
-            quantise(s, 0)
+        def round_pairs(s, u):
+            pairs[s, u] = keep.tile([P, T, 2], BF16, name=f"pairs{s}{u}", align_bytes=64)
+            src = raw[s, u][:].rearrange("p e w -> p w e")
+            v = VEC_COLS[s, u]
+            nc.vector.tensor_copy(pairs[s, u][:, 0:v, :], src[:, 0:v, :])
+            nc.scalar.copy(pairs[s, u][:, v:T, :], src[:, v:T, :])
+
+        round_pairs(0, 0)
+        gather(0, 0, 0)
+        gather(0, 0, 1)
+        round_pairs(0, 1)
+        gather(0, 1, 0)
+        round_pairs(1, 0)
+        quantise(0, 0)
+        gather(0, 1, 1)
+        round_pairs(1, 1)
+        gather(1, 0, 0)
+        gather(1, 1, 0)
+        quantise(1, 0)
+        quantise(0, 1)
+        gather(1, 0, 1)
+        gather(1, 1, 1)
+        quantise(1, 1)
 
         def stage1(j):
             e, c0 = j * P // C, j * P % C
@@ -148,7 +154,7 @@ def tile_moe_res_glu_silu_kernel(
                     lhsT=xq[s, e][:, cols].bitcast(FP8X4),
                     lhsT_scale=xs[s, e][:, cols],
                     rhs=wt[e, m][:, s, 2 * KP * g : 2 * KP * (g + 1)].bitcast(FP4X4),
-                    rhs_scale=wsc[e, m][:, s, g * KP : (g + 1) * KP],
+                    rhs_scale=wsc[m][:, e, s, g * KP : (g + 1) * KP],
                     start=(s == 0),
                     stop=(s == PASSES - 1),
                 )
@@ -164,8 +170,7 @@ def tile_moe_res_glu_silu_kernel(
                 )
             return h
 
-        def stage2(j, h, y_sb):
-            e = j * P // C
+        def turn(h):
             turned = psum.tile([P, G, 2, P], F32, name="turned", tag="turned", bufs=2)
             hq_in = ring.tile([P, G, P, 4], BF16, name="hq_in", align_bytes=64)
             hq = ring.tile([P, G, P], U32, name="hq", align_bytes=64)
@@ -184,6 +189,10 @@ def tile_moe_res_glu_silu_kernel(
                 scales=hs[:].rearrange("p g r -> p (g r)"),
                 in_=hq_in[:].rearrange("p g r t -> p (g r t)"),
             )
+            return hq, hs
+
+        def stage2(j, hq, hs, y_sb):
+            e = j * P // C
             y = psum.tile([P, NT, P], F32, name="y", tag="y", bufs=1)
             for n in range(NT):
                 for g in range(G):
@@ -208,19 +217,15 @@ def tile_moe_res_glu_silu_kernel(
         ys = {j: keep.tile([P, NT, P], F32, name=f"ys{j}") for j in range(UNITS)}
         h = {}
         h[0] = stage1(0)
-        for s in range(PASSES):
-            for u in range(2):
-                gather(s, u, 1)
-            quantise(s, 1)
-        h[1] = stage1(1)
-        stage2(0, h[0], ys[0])
-        h[2] = stage1(2)
-        stage2(1, h[1], ys[1])
-        h[3] = stage1(3)
-        stage2(2, h[2], ys[2])
-        stage2(3, h[3], ys[3])
-        for j in range(UNITS):
-            scatter(ys[j], j)
+        turned_h = {}
+        for t in range(1, UNITS + 2):
+            if t < UNITS:
+                h[t] = stage1(t)
+            if t - 1 < UNITS:
+                turned_h[t - 1] = turn(h[t - 1])
+            if t >= 2:
+                stage2(t - 2, *turned_h[t - 2], ys[t - 2])
+                scatter(ys[t - 2], t - 2)
 
         for n in range(NT):
             done = keep.tile([P, T], F32, name=f"done{n}")

@@ -24,7 +24,7 @@ PASSES = K // KP
 G = H // KP
 UNITS = SLOTS // P
 NT = N // P
-VEC_COLS = {(0, 0): 384, (0, 1): 256, (1, 0): 256, (1, 1): 384}
+VEC_COLS = {(0, 0): 512, (0, 1): 256, (1, 0): 256, (1, 1): 384}
 
 
 def tile_moe_res_glu_silu_kernel(
@@ -37,7 +37,6 @@ def tile_moe_res_glu_silu_kernel(
         psum = ctx.enter_context(tc.psum_pool(name="psum", bufs=1))
 
         offsets = keep.tile([P, SLOTS // 16], U16, name="offsets")
-        nc.sync.dma_start(offsets[:], offs)
 
         warm = keep.tile([P, 1], F32, name="warm")
         nc.vector.memset(warm[:], 0.0)
@@ -77,6 +76,7 @@ def tile_moe_res_glu_silu_kernel(
             nc.sync.dma_start(wt[e, m][:].bitcast(I32), words[m][e].rearrange("s p b -> p s b").bitcast(I32))
 
         load_x(0, 0)
+        nc.sync.dma_start(offsets[:], offs)
         load_scales(w2sc, w2_scales)
         load_x(0, 1)
         load_x(1, 0)
@@ -229,5 +229,6 @@ def tile_moe_res_glu_silu_kernel(
 
         for n in range(NT):
             done = keep.tile([P, T], F32, name=f"done{n}")
-            nc.vector.tensor_tensor(done[:], back[n][:], res_in[n][:], ADD)
-            nc.sync.dma_start(out[n * P : (n + 1) * P, :], done[:])
+            for cols in (slice(0, 512), slice(512, T)):
+                nc.vector.tensor_tensor(done[:, cols], back[n][:, cols], res_in[n][:, cols], ADD)
+                nc.sync.dma_start(out[n * P : (n + 1) * P, cols], done[:, cols])

from contextlib import ExitStack

import concourse.mybir as mybir
from concourse.masks import make_identity

K, T, E, C, H, N = 1024, 768, 2, 256, 1024, 256
SLOTS = E * C
FLOPS = 2 * SLOTS * (2 * K * H + H * N)

F32 = mybir.dt.float32
BF16 = mybir.dt.bfloat16
U32 = mybir.dt.uint32
I32 = mybir.dt.int32
U16 = mybir.dt.uint16
U8 = mybir.dt.uint8
FP8X4 = mybir.dt.float8_e4m3fn_x4
FP4X4 = mybir.dt.float4_e2m1fn_x4
MULT, ADD = mybir.AluOpType.mult, mybir.AluOpType.add
SILU = mybir.ActivationFunctionType.Silu

P = 128
KP = 512
PASSES = K // KP
G = H // KP
UNITS = SLOTS // P
NT = N // P
VEC_COLS = {(0, 0): 512, (0, 1): 256, (1, 0): 256, (1, 1): 384}


def tile_moe_res_glu_silu_kernel(
    tc, xT, xr, w1_words, w1_scales, w3_words, w3_scales, w2_words, w2_scales, gate, offs, out
):
    nc = tc.nc
    with ExitStack() as ctx:
        keep = ctx.enter_context(tc.tile_pool(name="keep", bufs=1))
        ring = ctx.enter_context(tc.tile_pool(name="ring", bufs=2))
        psum = ctx.enter_context(tc.psum_pool(name="psum", bufs=1))

        offsets = keep.tile([P, SLOTS // 16], U16, name="offsets")

        warm = keep.tile([P, 1], F32, name="warm")
        nc.vector.memset(warm[:], 0.0)
        nc.scalar.activation(warm[:], warm[:], SILU)
        ident = keep.tile([P, P], F32, name="ident")
        make_identity(nc, ident[:])
        words = (w1_words, w3_words)
        w2sc = keep.tile([P, E, PASSES, N], U8, name="w2sc", align_bytes=64)
        nc.vector.memset(w2sc[:].rearrange("p e s n -> p (e s n)").bitcast(I32), 0)
        wsc = {}
        for m in range(2):
            wsc[m] = keep.tile([P, E, PASSES, H], U8, name=f"wsc{m}", align_bytes=64)
            nc.vector.memset(wsc[m][:].rearrange("p e s i -> p (e s i)").bitcast(I32), 0)
        back = {}
        for n in range(NT):
            back[n] = keep.tile([P, T], F32, name=f"back{n}")
            nc.vector.memset(back[n][:], 0.0)

        def load_scales(plane, scales):
            for q in range(4):
                nc.sync.dma_start(
                    plane[32 * q : 32 * q + 4].rearrange("p e s i -> p (e s) i").bitcast(I32),
                    scales[:, :, 4 * q : 4 * q + 4, :].rearrange("e s q i -> q (e s) i").bitcast(I32),
                )

        xview = xT.rearrange("(s p u e) w -> s u p e w", s=PASSES, p=P, u=2, e=2)
        raw = {}

        def load_x(s, u):
            raw[s, u] = keep.tile([P, 2, T], F32, name=f"raw{s}{u}")
            nc.sync.dma_start(raw[s, u][:], xview[s, u])

        wt = {}

        def load_words(e, m):
            wt[e, m] = keep.tile([P, PASSES, 2 * H], U8, name=f"wt{e}{m}", align_bytes=64)
            nc.sync.dma_start(wt[e, m][:].bitcast(I32), words[m][e].rearrange("s p b -> p s b").bitcast(I32))

        load_x(0, 0)
        nc.sync.dma_start(offsets[:], offs)
        load_scales(w2sc, w2_scales)
        load_x(0, 1)
        load_x(1, 0)
        load_x(1, 1)
        load_scales(wsc[0], w1_scales)
        load_words(0, 0)
        load_words(0, 1)
        load_scales(wsc[1], w3_scales)
        w2t = keep.tile([P, E, PASSES, 2 * N], U8, name="w2t", align_bytes=64)
        nc.sync.dma_start(w2t[:].bitcast(I32), w2_words.rearrange("e s p b -> p e s b").bitcast(I32))
        load_words(1, 0)
        load_words(1, 1)
        gates = keep.tile([P, SLOTS], F32, name="gates")
        nc.sync.dma_start(gates[:], gate[0:P, :])
        res_in = {}
        for n in range(NT):
            res_in[n] = keep.tile([P, T], F32, name=f"res_in{n}")
            nc.sync.dma_start(res_in[n][:], xr[n * P : (n + 1) * P, :])

        xq, xs, grouped, pairs = {}, {}, {}, {}
        for s in range(PASSES):
            for e in range(E):
                grouped[s, e] = keep.tile([P, C, 4], BF16, name=f"grouped{s}{e}", align_bytes=64)
                xq[s, e] = keep.tile([P, C], U32, name=f"xq{s}{e}", align_bytes=64)
                xs[s, e] = keep.tile([P, C], U8, name=f"xs{s}{e}", align_bytes=64)

        def gather(s, u, e):
            pair_out = grouped[s, e][:].rearrange("p r t -> p (r t)").bitcast(U32).rearrange("p (r u) -> p r u", u=2)
            table = pairs[s, u][:].rearrange("p w e -> p (w e)").bitcast(U32)
            nc.vector.tensor_copy(pair_out[:, :, u], table.indirect(offsets[:, e * C // 16 : (e + 1) * C // 16]))

        def quantise(s, e):
            nc.vector.quantize_mx(
                out=xq[s, e][:].bitcast(FP8X4), scales=xs[s, e][:], in_=grouped[s, e][:].rearrange("p r t -> p (r t)")
            )

        def round_pairs(s, u):
            pairs[s, u] = keep.tile([P, T, 2], BF16, name=f"pairs{s}{u}", align_bytes=64)
            src = raw[s, u][:].rearrange("p e w -> p w e")
            v = VEC_COLS[s, u]
            nc.vector.tensor_copy(pairs[s, u][:, 0:v, :], src[:, 0:v, :])
            nc.scalar.copy(pairs[s, u][:, v:T, :], src[:, v:T, :])

        round_pairs(0, 0)
        gather(0, 0, 0)
        gather(0, 0, 1)
        round_pairs(0, 1)
        gather(0, 1, 0)
        round_pairs(1, 0)
        quantise(0, 0)
        gather(0, 1, 1)
        round_pairs(1, 1)
        gather(1, 0, 0)
        gather(1, 1, 0)
        quantise(1, 0)
        quantise(0, 1)
        gather(1, 0, 1)
        gather(1, 1, 1)
        quantise(1, 1)

        def stage1(j):
            e, c0 = j * P // C, j * P % C
            cols = slice(c0, c0 + P)
            acc = {}
            for g in range(G):
                for m in range(2):
                    acc[g, m] = psum.tile([P, KP], F32, name=f"acc{g}{m}", tag="acc", bufs=5)
            if j == 0:
                order = [(g, m, s) for s in range(PASSES) for g in range(G) for m in range(2)]
            else:
                order = [(g, m, s) for g in range(G) for m in range(2) for s in range(PASSES)]
            for g, m, s in order:
                nc.tensor.matmul_mx(
                    out=acc[g, m][:],
                    lhsT=xq[s, e][:, cols].bitcast(FP8X4),
                    lhsT_scale=xs[s, e][:, cols],
                    rhs=wt[e, m][:, s, 2 * KP * g : 2 * KP * (g + 1)].bitcast(FP4X4),
                    rhs_scale=wsc[m][:, e, s, g * KP : (g + 1) * KP],
                    start=(s == 0),
                    stop=(s == PASSES - 1),
                )
            h = ring.tile([P, G, 2, P, 2], BF16, name="h", align_bytes=64)
            for g in range(G):
                act = ring.tile([P, KP], F32, name="act", bufs=3)
                nc.scalar.activation(act[:], acc[g, 0][:], SILU)
                nc.vector.tensor_tensor(
                    h[:, g, :, :, :],
                    act[:].rearrange("r (p u e) -> r u p e", u=2, e=2),
                    acc[g, 1][:].rearrange("r (p u e) -> r u p e", u=2, e=2),
                    MULT,
                )
            return h

        def turn(h):
            turned = psum.tile([P, G, 2, P], F32, name="turned", tag="turned", bufs=2)
            hq_in = ring.tile([P, G, P, 4], BF16, name="hq_in", align_bytes=64)
            hq = ring.tile([P, G, P], U32, name="hq", align_bytes=64)
            hs = ring.tile([P, G, P], U8, name="hs", align_bytes=64)
            hw = h[:].rearrange("r g u p e -> r (g u p e)").bitcast(F32)
            for g in range(G):
                for u in range(2):
                    w0 = (2 * g + u) * P
                    nc.tensor.transpose(turned[:, g, u, :], hw[:, w0 : w0 + P], ident[:])
            nc.scalar.copy(
                hq_in[:].rearrange("p g r t -> p (g r t)").bitcast(F32).rearrange("p (g r u) -> p g r u", g=G, u=2),
                turned[:].rearrange("p g u r -> p g r u"),
            )
            nc.vector.quantize_mx(
                out=hq[:].rearrange("p g r -> p (g r)").bitcast(FP8X4),
                scales=hs[:].rearrange("p g r -> p (g r)"),
                in_=hq_in[:].rearrange("p g r t -> p (g r t)"),
            )
            return hq, hs

        def stage2(j, hq, hs, y_sb):
            e = j * P // C
            y = psum.tile([P, NT, P], F32, name="y", tag="y", bufs=1)
            for n in range(NT):
                for g in range(G):
                    nc.tensor.matmul_mx(
                        out=y[:, n, :],
                        lhsT=w2t[:, e, g, 2 * P * n : 2 * P * (n + 1)].bitcast(FP4X4),
                        lhsT_scale=w2sc[:, e, g, P * n : P * (n + 1)],
                        rhs=hq[:, g, :].bitcast(FP8X4),
                        rhs_scale=hs[:, g, :],
                        start=(g == 0),
                        stop=(g == G - 1),
                    )
            nc.scalar.copy(y_sb[:], y[:])

        def scatter(y_sb, j):
            cols = slice(j * P, (j + 1) * P)
            for n in range(NT):
                nc.vector.tensor_tensor(
                    back[n][:].indirect(offsets[:, j * P // 16 : (j + 1) * P // 16]), y_sb[:, n, :], gates[:, cols], MULT
                )

        ys = {j: keep.tile([P, NT, P], F32, name=f"ys{j}") for j in range(UNITS)}
        h = {}
        h[0] = stage1(0)
        turned_h = {}
        for t in range(1, UNITS + 2):
            if t < UNITS:
                h[t] = stage1(t)
            if t - 1 < UNITS:
                turned_h[t - 1] = turn(h[t - 1])
            if t >= 2:
                stage2(t - 2, *turned_h[t - 2], ys[t - 2])
                scatter(ys[t - 2], t - 2)

        for n in range(NT):
            done = keep.tile([P, T], F32, name=f"done{n}")
            for cols in (slice(0, 512), slice(512, T)):
                nc.vector.tensor_tensor(done[:, cols], back[n][:, cols], res_in[n][:, cols], ADD)
                nc.sync.dma_start(out[n * P : (n + 1) * P, cols], done[:, cols])
